import numpy as np
import ml_dtypes


def mxq(x, axis, fmt="e4m3"):
    dtype, down = {"e4m3": (ml_dtypes.float8_e4m3fn, 7), "e5m2": (ml_dtypes.float8_e5m2, 14)}[fmt]
    v = np.moveaxis(np.asarray(x, np.float32).astype(ml_dtypes.bfloat16).astype(np.float64), axis, -1)
    blocks = v.reshape(v.shape[:-1] + (-1, 32))
    amax = np.abs(blocks).max(-1, keepdims=True)
    byte = np.maximum(np.where(amax > 0, np.frexp(amax)[1] - 1 + 127, 0) - down, 1)
    scale = np.exp2(byte - 127.0)
    codes = (blocks / scale).astype(np.float32).astype(dtype).astype(np.float64)
    return np.moveaxis((codes * scale).reshape(v.shape), -1, axis)


WIDE = False


def mx_kscale(k):
    if not WIDE:
        return np.ones(k)
    levels = np.array([18, -18])
    if k % 512:
        return np.exp2(np.random.permutation(np.resize(levels, k // 32))).repeat(32)
    a = np.empty((k // 512, 16))
    for p in range(k // 512):
        a[p, :8] = np.random.permutation(np.resize(levels, 8))
        for g in range(8):
            far = levels[np.abs(levels - a[p, g]) >= 10]
            a[p, g + 8] = far[np.random.randint(len(far))]
    return np.exp2(a.ravel()).repeat(32)


def f64(x):
    return np.asarray(x).astype(np.float64)


def striped(idx):
    return np.tile(np.asarray(idx).reshape(-1, 16).T, (8, 1)).astype(np.uint16)


def unstriped(offs):
    return offs[:16].T.reshape(-1).astype(np.int64)


B, N, T, D, DV, R = 1, 512, 1024, 512, 512, 512


def setup_inputs():
    n = np.random.standard_normal
    idx = np.random.permutation(T)[:B * N]
    s = mx_kscale(D)[:, None]
    z = mx_kscale(R)[:, None]
    v = mx_kscale(DV)[:, None]
    q = n((B, D, R))
    do = n((B, DV, R))
    u = np.ones(T)
    u[idx] = mx_kscale(B * N)
    r = np.random.uniform(0.5, 2.0, T) * u
    return {
        "qT": (q * s).astype(np.float32),
        "kT": (n((D, T)) * (1.00 / np.sqrt(D)) / s / r).astype(np.float32),
        "vT": (n((DV, T)) / np.sqrt(DV) / v).astype(np.float32),
        "doT": (do * v).astype(np.float32),
        "rw": (np.random.uniform(0.5, 1.5, (B, R, 1)) * 1.0 / np.sqrt(R) * z).astype(np.float32),
        "ts": np.tile(r, (128, 1)).astype(np.float32),
        "qm": (q.transpose(0, 2, 1) / z).astype(np.float32),
        "dom": (do.transpose(0, 2, 1) / z).astype(np.float32),
        "offs": striped(idx),
    }


def reference(qT, kT, vT, doT, rw, ts, qm, dom, offs):
    idx = unstriped(offs)
    pick = lambda x: x[:, idx].reshape(x.shape[0], B, N).transpose(1, 0, 2)
    k = pick(f64(kT))
    a = mxq(f64(qT), 1, "e4m3").transpose(0, 2, 1) @ mxq(k, 1, "e4m3")
    ts_ = pick(f64(ts))[:, :1, :]
    a = a * ts_
    p = 1.0 / (1.0 + np.exp(-a))
    dp = mxq(f64(doT), 1, "e5m2").transpose(0, 2, 1) @ mxq(pick(f64(vT)), 1, "e4m3")
    ds = f64(rw) * dp * p * (1.0 - p)
    ds = ts_ * ds
    gq = mxq(ds, 2, "e5m2") @ mxq(k, 2, "e4m3").transpose(0, 2, 1)
    dk = mxq(f64(qm), 1, "e4m3").transpose(0, 2, 1) @ mxq(ds, 1, "e5m2")
    dv = mxq(f64(dom), 1, "e5m2").transpose(0, 2, 1) @ mxq(f64(rw) * p, 1, "e4m3")
    gk = np.zeros((D, T))
    gk[:, idx] = dk.transpose(1, 0, 2).reshape(D, B * N)
    gv = np.zeros((DV, T))
    gv[:, idx] = dv.transpose(1, 0, 2).reshape(DV, B * N)
    return gq, gk, gv

@@ -1,0 +1,258 @@
+from contextlib import ExitStack
+
+import concourse.mybir as mybir
+from concourse.masks import make_identity
+
+F32 = mybir.dt.float32
+BF16 = mybir.dt.bfloat16
+I32 = mybir.dt.int32
+U32 = mybir.dt.uint32
+U16 = mybir.dt.uint16
+U8 = mybir.dt.uint8
+E4M3 = mybir.dt.float8_e4m3fn_x4
+E5M2 = mybir.dt.float8_e5m2_x4
+ACT = mybir.ActivationFunctionType
+ALU = mybir.AluOpType
+
+P = 128
+PACK = 4
+N = 512
+T = 1024
+FLOPS = 5 * 2 * 512 * 512 * 512
+Q_SPLIT = 78
+DOM_SPLIT = 52
+
+
+def tile_attend_gat_sig_qkv_ts_kernel(tc, qT, kT, vT, doT, rw, ts, qm, dom, offs, out_0, out_1, out_2):
+    nc = tc.nc
+    with ExitStack() as ctx:
+        sb = ctx.enter_context(tc.tile_pool(name="sb", bufs=1))
+        ps = ctx.enter_context(tc.psum_pool(name="ps", bufs=1))
+
+        def alloc(name, shape, dtype):
+            return sb.tile(shape, dtype, name=name, align_bytes=64)
+
+        bank = [ps.tile([P, N], F32, name=f"bank{b}") for b in range(8)]
+
+        def quarter(b, j):
+            return bank[b][:, j * P : (j + 1) * P]
+
+        def load_rows(name, src):
+            raw = alloc(name, [P, PACK, N], F32)
+            nc.sync.dma_start(out=raw[:], in_=src.rearrange("(p j) c -> p j c", j=PACK))
+            return raw
+
+        def load_pool_piece(name, pool, u, h):
+            raw = alloc(name, [P, 2, N], F32)
+            rows = pool.rearrange("(p j) c -> p j c", j=PACK)
+            nc.sync.dma_start(out=raw[:], in_=rows[:, 2 * u : 2 * u + 2, h * N : (h + 1) * N])
+            return raw
+
+        k_raw = {}
+        k_raw[0, 0] = load_pool_piece("k_raw00", kT, 0, 0)
+        offsets = sb.tile([P, N // 16], U16, name="offsets")
+        nc.sync.dma_start(offsets[:], offs)
+        ts_pool = alloc("ts_pool", [P, T], F32)
+        nc.sync.dma_start(out=ts_pool[0:32, :], in_=ts[0:32, :])
+        rw_col = alloc("rw_col", [P, PACK], F32)
+        nc.sync.dma_start(out=rw_col[:], in_=rw[0].rearrange("(s t) o -> s (t o)", t=PACK))
+        for u, h in ((0, 1), (1, 0), (1, 1)):
+            k_raw[u, h] = load_pool_piece(f"k_raw{u}{h}", kT, u, h)
+        q_raw = load_rows("q_raw", qT[0])
+        dom_raw = load_rows("dom_raw", dom[0])
+        v_raw = {}
+        for u in range(2):
+            for h in range(2):
+                v_raw[u, h] = load_pool_piece(f"v_raw{u}{h}", vT, u, h)
+        do_raw = load_rows("do_raw", doT[0])
+        qm_raw = load_rows("qm_raw", qm[0])
+
+        ident = alloc("ident", [P, P], F32)
+        make_identity(nc, ident[:])
+        nc.vector.memset(ts_pool[32:64, :], 0.0)
+        nc.vector.memset(ts_pool[64:128, :], 0.0)
+        warm = alloc("warm", [P, 2], F32)
+        nc.vector.memset(warm[:, 0:1], 0.0)
+        nc.scalar.activation(out=warm[:, 1:2], in_=warm[:, 0:1], func=ACT.Sigmoid)
+        window = [alloc(f"window{w}", [P, T], F32) for w in range(4)]
+        for w in range(4):
+            nc.gpsimd.memset(window[w][:], 0.0)
+
+        def operand(name):
+            return (alloc(name + "_bf", [P, N * PACK], BF16), alloc(name + "_codes", [P, N], U32), alloc(name + "_scales", [P, N], U8))
+
+        def quantize(op, fmt, lo=0, hi=N):
+            bf, codes, scales = op
+            nc.vector.quantize_mx(out=codes[:, lo:hi].bitcast(fmt), scales=scales[:, lo:hi], in_=bf[:, lo * PACK : hi * PACK])
+
+        def product(b, stat, stat_fmt, m, mov, mov_fmt):
+            cols = slice(m * P, (m + 1) * P)
+            nc.tensor.matmul_mx(out=bank[b][:], lhsT=stat[1][:, cols].bitcast(stat_fmt), lhsT_scale=stat[2][:, cols],
+                                rhs=mov[1][:].bitcast(mov_fmt), rhs_scale=mov[2][:], start=True, stop=True)
+
+        for t in range(PACK):
+            nc.tensor.transpose(quarter(4, t), rw_col[:, t : t + 1].to_broadcast([P, P]), ident[:])
+        ts_listed = alloc("ts_listed", [P, N], F32)
+        nc.vector.tensor_copy(ts_listed[:], ts_pool[:].indirect(offsets[:]))
+        for t in range(PACK):
+            nc.tensor.transpose(quarter(5, t), ts_listed[:, t:N:PACK], ident[:])
+        ts_col = alloc("ts_col", [P, PACK], F32)
+        neg_ts_col = alloc("neg_ts_col", [P, PACK], F32)
+        nc.vector.tensor_copy(ts_col[:], bank[5][:, 0:N:P])
+        nc.vector.tensor_scalar(neg_ts_col[:], bank[5][:, 0:N:P], -1.0, None, ALU.mult)
+
+        def cast_pairs(pairs, raw, h, on_vector):
+            dst = pairs[:, h * N : (h + 1) * N].bitcast(BF16).rearrange("p (c e) -> p c e", e=2)
+            src = raw[:].rearrange("p e c -> p c e")
+            if on_vector:
+                nc.vector.tensor_copy(dst, src)
+            else:
+                nc.scalar.activation(out=dst, in_=src, func=ACT.Copy)
+
+        def gather_pool(name, raw, op, vector_piece):
+            listed = alloc(name + "_listed", [P, 2, N], U32)
+            for u in range(2):
+                pairs = alloc(f"{name}_pairs{u}", [P, T], U32)
+                for h in range(2):
+                    cast_pairs(pairs, raw[u, h], h, (u, h) == vector_piece)
+                nc.vector.tensor_copy(listed[:, u, :], pairs[:].indirect(offsets[:]))
+            word, copy = (U32, nc.scalar.copy) if vector_piece is None else (I32, nc.vector.tensor_copy)
+            copy(
+                op[0][:].bitcast(word).rearrange("p (t s u) -> p s t u", t=PACK, u=2),
+                listed[:].bitcast(word).rearrange("p u (s t) -> p s t u", t=PACK),
+            )
+
+        k_op = operand("k")
+        gather_pool("k", k_raw, k_op, (1, 1))
+        q_op = operand("q")
+        q_dst = q_op[0][:].rearrange("p (t s j) -> p s j t", t=PACK, j=PACK)
+        q_src = q_raw[:].rearrange("p j (s t) -> p s j t", t=PACK)
+        nc.scalar.copy(q_dst[:, :Q_SPLIT], q_src[:, :Q_SPLIT])
+        nc.vector.tensor_copy(q_dst[:, Q_SPLIT:], q_src[:, Q_SPLIT:])
+        quantize(k_op, E4M3)
+        quantize(q_op, E4M3)
+
+        def interleave(copy, op, raw, lo, hi):
+            dst = op[0][:].rearrange("p (c i j) -> p c j i", i=PACK, j=PACK)
+            src = raw[:].rearrange("p j (c i) -> p c j i", i=PACK)
+            copy(dst[:, lo:hi], src[:, lo:hi])
+
+        prob = [alloc(f"prob{t}", [P, N], F32) for t in range(PACK)]
+        pw32 = [alloc(f"pw32_{t}", [P, N], F32) for t in range(PACK)]
+        slope = [alloc(f"slope{t}", [P, N], F32) for t in range(PACK)]
+        pw_op = operand("pw")
+        dom_op = operand("dom")
+        for t in range(PACK):
+            product(t, k_op, E4M3, t, q_op, E4M3)
+        for t in range(PACK):
+            nc.scalar.activation(out=prob[t][:], in_=bank[t][:], func=ACT.Sigmoid, scale=ts_col[:, t : t + 1])
+            nc.vector.tensor_tensor(pw32[t][:], prob[t][:], bank[4][:], ALU.mult)
+        for t in range(PACK):
+            for j in range(PACK):
+                nc.tensor.transpose(quarter(t, j), pw32[t][:, j * P : (j + 1) * P], ident[:])
+            nc.scalar.copy(
+                pw_op[0][:, t * N : (t + 1) * N].rearrange("s (p j) -> s p j", j=PACK),
+                bank[t][:].rearrange("s (j p) -> s p j", j=PACK),
+            )
+            quantize(pw_op, E4M3, t * P, (t + 1) * P)
+        interleave(nc.scalar.copy, dom_op, dom_raw, 0, DOM_SPLIT)
+        interleave(nc.vector.tensor_copy, dom_op, dom_raw, DOM_SPLIT, P)
+        quantize(dom_op, E5M2)
+
+        stage = [alloc(f"stage{m}", [P, N], F32) for m in range(PACK)]
+
+        def to_list_order(m, b):
+            nc.scalar.copy(stage[m][:].rearrange("e (p t) -> e p t", t=PACK), bank[b][:].rearrange("e (t p) -> e p t", t=PACK))
+
+        def scatter(m, out):
+            nc.vector.tensor_copy(window[m][:].indirect(offsets[:]), stage[m][:])
+            nc.sync.dma_start(out=out[m * P : (m + 1) * P, :], in_=window[m][:])
+
+        for m in range(2):
+            product(5 + m, dom_op, E5M2, m, pw_op, E4M3)
+            to_list_order(m, 5 + m)
+        for t in range(PACK):
+            nc.vector.scalar_tensor_tensor(slope[t][:], prob[t][:], 1.0, pw32[t][:], ALU.subtract, ALU.mult)
+        scatter(0, out_2)
+        scatter(1, out_2)
+
+        v_op = operand("v")
+        gather_pool("v", v_raw, v_op, None)
+        do_op = operand("do")
+        do_dst = do_op[0][:].rearrange("p (u s e j) -> p s j u e", u=2, e=2, j=PACK)
+        do_src = do_raw[:].rearrange("p j (s u e) -> p s j u e", u=2, e=2)
+        for a in range(2):
+            nc.scalar.copy(do_dst[:, a * 64 : (a + 1) * 64], do_src[:, a * 64 : (a + 1) * 64])
+        qm_op = operand("qm")
+        interleave(nc.scalar.copy, qm_op, qm_raw, 0, 64)
+        interleave(nc.scalar.copy, qm_op, qm_raw, 64, P)
+        quantize(do_op, E5M2)
+        quantize(v_op, E4M3)
+        quantize(qm_op, E4M3)
+
+        kt_op = operand("kt")
+        k_words = k_op[0][:].bitcast(F32).rearrange("p (t s u) -> p t u s", t=PACK, u=2)
+        for u in range(2):
+            for t in range(PACK):
+                nc.tensor.transpose(quarter(5 + u, t), k_words[:, t, u, :], ident[:])
+            nc.scalar.copy(
+                kt_op[0][:].rearrange("s (p u e t) -> s u p e t", u=2, e=2, t=PACK)[:, u],
+                bank[5 + u][:].bitcast(BF16).rearrange("s (t p e) -> s p e t", t=PACK, e=2),
+            )
+
+        ds_flat = alloc("ds", [P, PACK * N], BF16)
+        ds = ds_flat[:].rearrange("p (t c) -> p t c", t=PACK)
+        dsr_op = operand("dsr")
+        for t in range(PACK):
+            product(t, v_op, E4M3, t, do_op, E5M2)
+        for t in range(PACK):
+            for u in range(2):
+                half = slice(u * 256, (u + 1) * 256)
+                nc.vector.scalar_tensor_tensor(
+                    ds[:, t, half].rearrange("p (s e) -> p s e", e=2),
+                    bank[t][:, half].rearrange("p (s e) -> p s e", e=2),
+                    neg_ts_col[:, t : t + 1],
+                    slope[t][:, half].rearrange("p (e s) -> p s e", e=2),
+                    ALU.mult,
+                    ALU.mult,
+                )
+        ds_bank = (4, 7)
+        for h in range(2):
+            for t2 in range(2):
+                words = ds_flat[:, (2 * h + t2) * N : (2 * h + t2 + 1) * N].bitcast(F32)
+                for u in range(2):
+                    nc.tensor.transpose(quarter(ds_bank[h], 2 * t2 + u), words[:, u * P : (u + 1) * P], ident[:])
+            nc.scalar.copy(
+                dsr_op[0][:, h * 1024 : (h + 1) * 1024].bitcast(F32).rearrange("s (t p u) -> s t p u", t=2, u=2),
+                bank[ds_bank[h]][:].rearrange("s (t u p) -> s t p u", t=2, u=2),
+            )
+        product(0, dom_op, E5M2, 2, pw_op, E4M3)
+        to_list_order(2, 0)
+        scatter(2, out_2)
+        quantize(dsr_op, E5M2)
+        product(7, dom_op, E5M2, 3, pw_op, E4M3)
+        to_list_order(3, 7)
+        scatter(3, out_2)
+
+        dss_op = operand("dss")
+        for u in range(2):
+            nc.scalar.copy(
+                dss_op[0][:, u * 1024 : (u + 1) * 1024].rearrange("p (e s t) -> p s t e", e=2, t=PACK),
+                ds[:, :, u * 256 : (u + 1) * 256].rearrange("p t (s e) -> p s t e", e=2),
+            )
+        quantize(kt_op, E4M3)
+        quantize(dss_op, E5M2)
+
+        for m in range(PACK):
+            product(1 + m, qm_op, E4M3, m, dsr_op, E5M2)
+            to_list_order(m, 1 + m)
+            scatter(m, out_1)
+
+        gq = alloc("gq", [P, PACK, N], F32)
+        gq_bank = (5, 6, 7, 0)
+        rows = out_0[0].rearrange("(s m) d -> s m d", m=PACK)
+        for m in range(PACK):
+            product(gq_bank[m], dss_op, E5M2, m, kt_op, E4M3)
+            nc.scalar.copy(gq[:, m, :], bank[gq_bank[m]][:])
+            if m % 2 == 1:
+                nc.scalar.dma_start(out=rows[:, m - 1 : m + 1, :], in_=gq[:, m - 1 : m + 1, :])

@@ -18,9 +18,12 @@ P = 128
 PACK = 4
 N = 512
 T = 1024
+HALF = N // 2
 FLOPS = 5 * 2 * 512 * 512 * 512
-Q_SPLIT = 78
-DOM_SPLIT = 52
+K_SPLIT = 176
+GPSIMD_TILES = 3
+V_SPLIT = 304
+Q_SPLIT = 88
 
 
 def tile_attend_gat_sig_qkv_ts_kernel(tc, qT, kT, vT, doT, rw, ts, qm, dom, offs, out_0, out_1, out_2):
@@ -29,8 +32,8 @@ def tile_attend_gat_sig_qkv_ts_kernel(tc, qT, kT, vT, doT, rw, ts, qm, dom, offs
         sb = ctx.enter_context(tc.tile_pool(name="sb", bufs=1))
         ps = ctx.enter_context(tc.psum_pool(name="ps", bufs=1))
 
-        def alloc(name, shape, dtype):
-            return sb.tile(shape, dtype, name=name, align_bytes=64)
+        def alloc(name, shape, dtype, tag=""):
+            return sb.tile(shape, dtype, name=name, align_bytes=64, tag=tag or name)
 
         bank = [ps.tile([P, N], F32, name=f"bank{b}") for b in range(8)]
 
@@ -43,27 +46,29 @@ def tile_attend_gat_sig_qkv_ts_kernel(tc, qT, kT, vT, doT, rw, ts, qm, dom, offs
             return raw
 
         def load_pool_piece(name, pool, u, h):
-            raw = alloc(name, [P, 2, N], F32)
+            raw = alloc(f"{name}_raw{u}{h}", [P, 2, N], F32)
             rows = pool.rearrange("(p j) c -> p j c", j=PACK)
             nc.sync.dma_start(out=raw[:], in_=rows[:, 2 * u : 2 * u + 2, h * N : (h + 1) * N])
             return raw
 
         k_raw = {}
-        k_raw[0, 0] = load_pool_piece("k_raw00", kT, 0, 0)
+        v_raw = {}
+        k_raw[0, 0] = load_pool_piece("k", kT, 0, 0)
         offsets = sb.tile([P, N // 16], U16, name="offsets")
         nc.sync.dma_start(offsets[:], offs)
+        k_raw[0, 1] = load_pool_piece("k", kT, 0, 1)
         ts_pool = alloc("ts_pool", [P, T], F32)
         nc.sync.dma_start(out=ts_pool[0:32, :], in_=ts[0:32, :])
         rw_col = alloc("rw_col", [P, PACK], F32)
         nc.sync.dma_start(out=rw_col[:], in_=rw[0].rearrange("(s t) o -> s (t o)", t=PACK))
-        for u, h in ((0, 1), (1, 0), (1, 1)):
-            k_raw[u, h] = load_pool_piece(f"k_raw{u}{h}", kT, u, h)
+        for h in range(2):
+            k_raw[1, h] = load_pool_piece("k", kT, 1, h)
         q_raw = load_rows("q_raw", qT[0])
+        for h in range(2):
+            v_raw[0, h] = load_pool_piece("v", vT, 0, h)
         dom_raw = load_rows("dom_raw", dom[0])
-        v_raw = {}
-        for u in range(2):
-            for h in range(2):
-                v_raw[u, h] = load_pool_piece(f"v_raw{u}{h}", vT, u, h)
+        for h in range(2):
+            v_raw[1, h] = load_pool_piece("v", vT, 1, h)
         do_raw = load_rows("do_raw", doT[0])
         qm_raw = load_rows("qm_raw", qm[0])
 
@@ -78,8 +83,12 @@ def tile_attend_gat_sig_qkv_ts_kernel(tc, qT, kT, vT, doT, rw, ts, qm, dom, offs
         for w in range(4):
             nc.gpsimd.memset(window[w][:], 0.0)
 
-        def operand(name):
-            return (alloc(name + "_bf", [P, N * PACK], BF16), alloc(name + "_codes", [P, N], U32), alloc(name + "_scales", [P, N], U8))
+        def operand(name, bf_tag="", codes_tag="", scales_tag=""):
+            return (
+                alloc(name + "_bf", [P, N * PACK], BF16, bf_tag),
+                alloc(name + "_codes", [P, N], U32, codes_tag),
+                alloc(name + "_scales", [P, N], U8, scales_tag),
+            )
 
         def quantize(op, fmt, lo=0, hi=N):
             bf, codes, scales = op
@@ -87,66 +96,89 @@ def tile_attend_gat_sig_qkv_ts_kernel(tc, qT, kT, vT, doT, rw, ts, qm, dom, offs
 
         def product(b, stat, stat_fmt, m, mov, mov_fmt):
             cols = slice(m * P, (m + 1) * P)
-            nc.tensor.matmul_mx(out=bank[b][:], lhsT=stat[1][:, cols].bitcast(stat_fmt), lhsT_scale=stat[2][:, cols],
-                                rhs=mov[1][:].bitcast(mov_fmt), rhs_scale=mov[2][:], start=True, stop=True)
+            nc.tensor.matmul_mx(
+                out=bank[b][:],
+                lhsT=stat[1][:, cols].bitcast(stat_fmt),
+                lhsT_scale=stat[2][:, cols],
+                rhs=mov[1][:].bitcast(mov_fmt),
+                rhs_scale=mov[2][:],
+                start=True,
+                stop=True,
+            )
+
+        def scalar_move(dst, src):
+            nc.scalar.activation(out=dst, in_=src, func=ACT.Copy)
+
+        def gpsimd_cast(dst, src):
+            nc.gpsimd.tensor_scalar(dst, src, 1.0, 0.0, ALU.mult, ALU.add)
+
+        def cast_pairs(move, pairs, raw, h, lo=0, hi=N):
+            dst = pairs[:, h * N + lo : h * N + hi].bitcast(BF16).rearrange("p (c e) -> p c e", e=2)
+            move(dst, raw[:, :, lo:hi].rearrange("p e c -> p c e"))
+
+        def gather(dst, pool):
+            nc.vector.tensor_copy(dst, pool[:].indirect(offsets[:]))
+
+        def weave(copy, word, op, listed, lo=0, hi=PACK):
+            copy(
+                op[0][:].bitcast(word).rearrange("p (t s u) -> p s t u", t=PACK, u=2)[:, :, lo:hi],
+                listed[:].bitcast(word).rearrange("p (u s t) -> p s t u", u=2, t=PACK)[:, :, lo:hi],
+            )
+
+        def interleave(copy, bf, raw, lo, hi):
+            dst = bf[:].rearrange("p (c i j) -> p c j i", i=PACK, j=PACK)
+            src = raw[:].rearrange("p j (c i) -> p c j i", i=PACK)
+            copy(dst[:, lo:hi], src[:, lo:hi])
 
         for t in range(PACK):
             nc.tensor.transpose(quarter(4, t), rw_col[:, t : t + 1].to_broadcast([P, P]), ident[:])
         ts_listed = alloc("ts_listed", [P, N], F32)
-        nc.vector.tensor_copy(ts_listed[:], ts_pool[:].indirect(offsets[:]))
+        gather(ts_listed[:], ts_pool)
         for t in range(PACK):
             nc.tensor.transpose(quarter(5, t), ts_listed[:, t:N:PACK], ident[:])
-        ts_col = alloc("ts_col", [P, PACK], F32)
-        neg_ts_col = alloc("neg_ts_col", [P, PACK], F32)
-        nc.vector.tensor_copy(ts_col[:], bank[5][:, 0:N:P])
-        nc.vector.tensor_scalar(neg_ts_col[:], bank[5][:, 0:N:P], -1.0, None, ALU.mult)
 
-        def cast_pairs(pairs, raw, h, on_vector):
-            dst = pairs[:, h * N : (h + 1) * N].bitcast(BF16).rearrange("p (c e) -> p c e", e=2)
-            src = raw[:].rearrange("p e c -> p c e")
-            if on_vector:
-                nc.vector.tensor_copy(dst, src)
-            else:
-                nc.scalar.activation(out=dst, in_=src, func=ACT.Copy)
-
-        def gather_pool(name, raw, op, vector_piece):
-            listed = alloc(name + "_listed", [P, 2, N], U32)
-            for u in range(2):
-                pairs = alloc(f"{name}_pairs{u}", [P, T], U32)
-                for h in range(2):
-                    cast_pairs(pairs, raw[u, h], h, (u, h) == vector_piece)
-                nc.vector.tensor_copy(listed[:, u, :], pairs[:].indirect(offsets[:]))
-            word, copy = (U32, nc.scalar.copy) if vector_piece is None else (I32, nc.vector.tensor_copy)
-            copy(
-                op[0][:].bitcast(word).rearrange("p (t s u) -> p s t u", t=PACK, u=2),
-                listed[:].bitcast(word).rearrange("p u (s t) -> p s t u", t=PACK),
-            )
-
+        k_pairs = [alloc(f"k_pairs{u}", [P, T], U32) for u in range(2)]
+        k_listed = alloc("k_listed", [P, 2 * N], U32)
         k_op = operand("k")
-        gather_pool("k", k_raw, k_op, (1, 1))
+        cast_pairs(scalar_move, k_pairs[0], k_raw[0, 0], 0)
+        cast_pairs(scalar_move, k_pairs[0], k_raw[0, 1], 1)
+        gather(k_listed[:, :N], k_pairs[0])
+        cast_pairs(scalar_move, k_pairs[1], k_raw[1, 0], 0)
+        cast_pairs(scalar_move, k_pairs[1], k_raw[1, 1], 1, 0, K_SPLIT)
+        cast_pairs(nc.vector.tensor_copy, k_pairs[1], k_raw[1, 1], 1, K_SPLIT, N)
+        gather(k_listed[:, N:], k_pairs[1])
+        ts_col = alloc("ts_col", [P, PACK], F32)
+        nc.scalar.copy(ts_col[:], bank[5][:, 0:N:P])
+        for a in range(2):
+            weave(nc.vector.tensor_copy, I32, k_op, k_listed, 2 * a, 2 * a + 2)
+        for a in range(2):
+            quantize(k_op, E4M3, a * HALF, (a + 1) * HALF)
         q_op = operand("q")
         q_dst = q_op[0][:].rearrange("p (t s j) -> p s j t", t=PACK, j=PACK)
         q_src = q_raw[:].rearrange("p j (s t) -> p s j t", t=PACK)
         nc.scalar.copy(q_dst[:, :Q_SPLIT], q_src[:, :Q_SPLIT])
         nc.vector.tensor_copy(q_dst[:, Q_SPLIT:], q_src[:, Q_SPLIT:])
-        quantize(k_op, E4M3)
         quantize(q_op, E4M3)
 
-        def interleave(copy, op, raw, lo, hi):
-            dst = op[0][:].rearrange("p (c i j) -> p c j i", i=PACK, j=PACK)
-            src = raw[:].rearrange("p j (c i) -> p c j i", i=PACK)
-            copy(dst[:, lo:hi], src[:, lo:hi])
-
-        prob = [alloc(f"prob{t}", [P, N], F32) for t in range(PACK)]
-        pw32 = [alloc(f"pw32_{t}", [P, N], F32) for t in range(PACK)]
-        slope = [alloc(f"slope{t}", [P, N], F32) for t in range(PACK)]
-        pw_op = operand("pw")
+        prob_all = alloc("prob", [P, PACK * N], F32)
+        pw32_all = alloc("pw32", [P, PACK * N], F32)
+        prob = [prob_all[:, t * N : (t + 1) * N] for t in range(PACK)]
+        pw32 = [pw32_all[:, t * N : (t + 1) * N] for t in range(PACK)]
         dom_op = operand("dom")
+        dom_dst = dom_op[0][:].rearrange("p (c j) -> p c j", j=PACK)
+        dom_src = dom_raw[:].rearrange("p j c -> p c j")
+        for a in range(2):
+            gpsimd_cast(dom_dst[:, a * HALF : (a + 1) * HALF], dom_src[:, a * HALF : (a + 1) * HALF])
         for t in range(PACK):
             product(t, k_op, E4M3, t, q_op, E4M3)
         for t in range(PACK):
-            nc.scalar.activation(out=prob[t][:], in_=bank[t][:], func=ACT.Sigmoid, scale=ts_col[:, t : t + 1])
-            nc.vector.tensor_tensor(pw32[t][:], prob[t][:], bank[4][:], ALU.mult)
+            width = HALF if t == PACK - 1 else N
+            for lo in range(0, N, width):
+                cols = slice(lo, lo + width)
+                nc.scalar.activation(out=prob[t][:, cols], in_=bank[t][:, cols], func=ACT.Sigmoid, scale=ts_col[:, t : t + 1])
+                nc.vector.tensor_tensor(pw32[t][:, cols], prob[t][:, cols], bank[4][:, cols], ALU.mult)
+        quantize(dom_op, E5M2)
+        pw_op = operand("pw", scales_tag="dom_bf")
         for t in range(PACK):
             for j in range(PACK):
                 nc.tensor.transpose(quarter(t, j), pw32[t][:, j * P : (j + 1) * P], ident[:])
@@ -155,42 +187,88 @@ def tile_attend_gat_sig_qkv_ts_kernel(tc, qT, kT, vT, doT, rw, ts, qm, dom, offs
                 bank[t][:].rearrange("s (j p) -> s p j", j=PACK),
             )
             quantize(pw_op, E4M3, t * P, (t + 1) * P)
-        interleave(nc.scalar.copy, dom_op, dom_raw, 0, DOM_SPLIT)
-        interleave(nc.vector.tensor_copy, dom_op, dom_raw, DOM_SPLIT, P)
-        quantize(dom_op, E5M2)
 
-        stage = [alloc(f"stage{m}", [P, N], F32) for m in range(PACK)]
+        stage = [alloc("stage0", [P, N], F32)]
 
         def to_list_order(m, b):
             nc.scalar.copy(stage[m][:].rearrange("e (p t) -> e p t", t=PACK), bank[b][:].rearrange("e (t p) -> e p t", t=PACK))
 
-        def scatter(m, out):
-            nc.vector.tensor_copy(window[m][:].indirect(offsets[:]), stage[m][:])
+        def scatter(i, out, m):
+            nc.vector.tensor_copy(window[m][:].indirect(offsets[:]), stage[i][:])
             nc.sync.dma_start(out=out[m * P : (m + 1) * P, :], in_=window[m][:])
 
-        for m in range(2):
-            product(5 + m, dom_op, E5M2, m, pw_op, E4M3)
-            to_list_order(m, 5 + m)
-        for t in range(PACK):
-            nc.vector.scalar_tensor_tensor(slope[t][:], prob[t][:], 1.0, pw32[t][:], ALU.subtract, ALU.mult)
-        scatter(0, out_2)
-        scatter(1, out_2)
+        for m, b in enumerate((5, 6, 4)):
+            product(b, dom_op, E5M2, m, pw_op, E4M3)
+        to_list_order(0, 5)
 
+        v_pairs = [alloc("v_pairs0", [P, T], U32), alloc("v_pairs1", [P, T], U32, "pw_bf")]
+        v_listed = alloc("v_listed", [P, 2 * N], U32)
         v_op = operand("v")
-        gather_pool("v", v_raw, v_op, None)
+        for h in range(2):
+            cast_pairs(scalar_move, v_pairs[0], v_raw[0, h], h)
+        gather(v_listed[:, :N], v_pairs[0])
+        cast_pairs(scalar_move, v_pairs[1], v_raw[1, 0], 0, 0, V_SPLIT)
+        cast_pairs(nc.vector.tensor_copy, v_pairs[1], v_raw[1, 0], 0, V_SPLIT, N)
+        cast_pairs(nc.vector.tensor_copy, v_pairs[1], v_raw[1, 1], 1)
+        gather(v_listed[:, N:], v_pairs[1])
+        scatter(0, out_2, 0)
+        rest = alloc("rest", [P, PACK * N], F32, "v_raw11")
+        nc.gpsimd.tensor_scalar(rest[:], prob_all[:], -1.0, 1.0, ALU.mult, ALU.add)
+
+        def slopes(both, first):
+            cols = slice(first * N, (first + 2) * N)
+            nc.gpsimd.tensor_tensor(both[:], rest[:, cols], pw32_all[:, cols], ALU.mult)
+            return [both[:, :N], both[:, N:]]
+
+        slope = slopes(alloc("slope01", [P, 2 * N], F32), 0)
         do_op = operand("do")
         do_dst = do_op[0][:].rearrange("p (u s e j) -> p s j u e", u=2, e=2, j=PACK)
         do_src = do_raw[:].rearrange("p j (s u e) -> p s j u e", u=2, e=2)
+        qm_bf = alloc("qm_bf", [P, N * PACK], BF16)
+        weave(nc.scalar.copy, U32, v_op, v_listed)
+        quantize(v_op, E4M3)
         for a in range(2):
             nc.scalar.copy(do_dst[:, a * 64 : (a + 1) * 64], do_src[:, a * 64 : (a + 1) * 64])
-        qm_op = operand("qm")
-        interleave(nc.scalar.copy, qm_op, qm_raw, 0, 64)
-        interleave(nc.scalar.copy, qm_op, qm_raw, 64, P)
         quantize(do_op, E5M2)
-        quantize(v_op, E4M3)
+        slope.extend(slopes(alloc("slope23", [P, 2 * N], F32, "do_bf"), 2))
+        stage.append(alloc("stage1", [P, N], F32, "do_raw"))
+        to_list_order(1, 6)
+        scatter(1, out_2, 1)
+        for a in range(2):
+            interleave(nc.scalar.copy, qm_bf, qm_raw, a * 64, (a + 1) * 64)
+
+        ds_flat = alloc("ds", [P, PACK * N], BF16)
+        ds = ds_flat[:].rearrange("p (t c) -> p t c", t=PACK)
+        for t in range(PACK):
+            product(t, v_op, E4M3, t, do_op, E5M2)
+        for t in range(GPSIMD_TILES):
+            scaled = alloc(f"scaled{t}", [P, N], F32)
+            nc.scalar.activation(out=scaled[:], in_=bank[t][:], func=ACT.Copy, scale=ts_col[:, t : t + 1])
+            nc.gpsimd.tensor_tensor(
+                ds[:, t, :].rearrange("p (u s e) -> p u s e", u=2, e=2),
+                scaled[:].rearrange("p (u s e) -> p u s e", u=2, e=2),
+                slope[t].rearrange("p (u e s) -> p u s e", u=2, e=2),
+                ALU.mult,
+            )
+        for t in range(GPSIMD_TILES, PACK):
+            for u in range(2):
+                half = slice(u * HALF, (u + 1) * HALF)
+                nc.vector.scalar_tensor_tensor(
+                    ds[:, t, half].rearrange("p (s e) -> p s e", e=2),
+                    bank[t][:, half].rearrange("p (s e) -> p s e", e=2),
+                    ts_col[:, t : t + 1],
+                    slope[t][:, half].rearrange("p (e s) -> p s e", e=2),
+                    ALU.mult,
+                    ALU.mult,
+                )
+        stage.append(alloc("stage2", [P, N], F32, "v_raw11"))
+        stage.append(alloc("stage3", [P, N], F32))
+        to_list_order(2, 4)
+        scatter(2, out_2, 2)
+        qm_op = (qm_bf, alloc("qm_codes", [P, N], U32, "v_raw11"), alloc("qm_scales", [P, N], U8))
         quantize(qm_op, E4M3)
 
-        kt_op = operand("kt")
+        kt_op = operand("kt", codes_tag="qm_bf")
         k_words = k_op[0][:].bitcast(F32).rearrange("p (t s u) -> p t u s", t=PACK, u=2)
         for u in range(2):
             for t in range(PACK):
@@ -199,54 +277,36 @@ def tile_attend_gat_sig_qkv_ts_kernel(tc, qT, kT, vT, doT, rw, ts, qm, dom, offs
                 kt_op[0][:].rearrange("s (p u e t) -> s u p e t", u=2, e=2, t=PACK)[:, u],
                 bank[5 + u][:].bitcast(BF16).rearrange("s (t p e) -> s p e t", t=PACK, e=2),
             )
+        quantize(kt_op, E4M3)
 
-        ds_flat = alloc("ds", [P, PACK * N], BF16)
-        ds = ds_flat[:].rearrange("p (t c) -> p t c", t=PACK)
         dsr_op = operand("dsr")
-        for t in range(PACK):
-            product(t, v_op, E4M3, t, do_op, E5M2)
-        for t in range(PACK):
-            for u in range(2):
-                half = slice(u * 256, (u + 1) * 256)
-                nc.vector.scalar_tensor_tensor(
-                    ds[:, t, half].rearrange("p (s e) -> p s e", e=2),
-                    bank[t][:, half].rearrange("p (s e) -> p s e", e=2),
-                    neg_ts_col[:, t : t + 1],
-                    slope[t][:, half].rearrange("p (e s) -> p s e", e=2),
-                    ALU.mult,
-                    ALU.mult,
-                )
-        ds_bank = (4, 7)
-        for h in range(2):
+        for h, b in ((0, 7), (1, 4)):
             for t2 in range(2):
                 words = ds_flat[:, (2 * h + t2) * N : (2 * h + t2 + 1) * N].bitcast(F32)
                 for u in range(2):
-                    nc.tensor.transpose(quarter(ds_bank[h], 2 * t2 + u), words[:, u * P : (u + 1) * P], ident[:])
+                    nc.tensor.transpose(quarter(b, 2 * t2 + u), words[:, u * P : (u + 1) * P], ident[:])
             nc.scalar.copy(
                 dsr_op[0][:, h * 1024 : (h + 1) * 1024].bitcast(F32).rearrange("s (t p u) -> s t p u", t=2, u=2),
-                bank[ds_bank[h]][:].rearrange("s (t u p) -> s t p u", t=2, u=2),
+                bank[b][:].rearrange("s (t u p) -> s t p u", t=2, u=2),
             )
-        product(0, dom_op, E5M2, 2, pw_op, E4M3)
-        to_list_order(2, 0)
-        scatter(2, out_2)
         quantize(dsr_op, E5M2)
         product(7, dom_op, E5M2, 3, pw_op, E4M3)
         to_list_order(3, 7)
-        scatter(3, out_2)
+        scatter(3, out_2, 3)
 
-        dss_op = operand("dss")
+        dss_op = operand("dss", bf_tag="dsr_bf")
+        dss_dst = dss_op[0][:].rearrange("p (u e s t) -> p u s t e", u=2, e=2, t=PACK)
+        dss_src = ds_flat[:].rearrange("p (t u s e) -> p u s t e", t=PACK, u=2, e=2)
         for u in range(2):
-            nc.scalar.copy(
-                dss_op[0][:, u * 1024 : (u + 1) * 1024].rearrange("p (e s t) -> p s t e", e=2, t=PACK),
-                ds[:, :, u * 256 : (u + 1) * 256].rearrange("p t (s e) -> p s t e", e=2),
-            )
-        quantize(kt_op, E4M3)
+            for a in range(2):
+                nc.scalar.copy(dss_dst[:, u, a * 64 : (a + 1) * 64], dss_src[:, u, a * 64 : (a + 1) * 64])
         quantize(dss_op, E5M2)
 
         for m in range(PACK):
             product(1 + m, qm_op, E4M3, m, dsr_op, E5M2)
-            to_list_order(m, 1 + m)
-            scatter(m, out_1)
+            stage.append(alloc(f"stage{PACK + m}", [P, N], F32))
+            to_list_order(PACK + m, 1 + m)
+            scatter(PACK + m, out_1, m)
 
         gq = alloc("gq", [P, PACK, N], F32)
         gq_bank = (5, 6, 7, 0)

from contextlib import ExitStack

import concourse.mybir as mybir
from concourse.masks import make_identity

F32 = mybir.dt.float32
BF16 = mybir.dt.bfloat16
I32 = mybir.dt.int32
U32 = mybir.dt.uint32
U16 = mybir.dt.uint16
U8 = mybir.dt.uint8
E4M3 = mybir.dt.float8_e4m3fn_x4
E5M2 = mybir.dt.float8_e5m2_x4
ACT = mybir.ActivationFunctionType
ALU = mybir.AluOpType

P = 128
PACK = 4
N = 512
T = 1024
HALF = N // 2
FLOPS = 5 * 2 * 512 * 512 * 512
K_SPLIT = 176
GPSIMD_TILES = 3
V_SPLIT = 304
Q_SPLIT = 88


def tile_attend_gat_sig_qkv_ts_kernel(tc, qT, kT, vT, doT, rw, ts, qm, dom, offs, out_0, out_1, out_2):
    nc = tc.nc
    with ExitStack() as ctx:
        sb = ctx.enter_context(tc.tile_pool(name="sb", bufs=1))
        ps = ctx.enter_context(tc.psum_pool(name="ps", bufs=1))

        def alloc(name, shape, dtype, tag=""):
            return sb.tile(shape, dtype, name=name, align_bytes=64, tag=tag or name)

        bank = [ps.tile([P, N], F32, name=f"bank{b}") for b in range(8)]

        def quarter(b, j):
            return bank[b][:, j * P : (j + 1) * P]

        def load_rows(name, src):
            raw = alloc(name, [P, PACK, N], F32)
            nc.sync.dma_start(out=raw[:], in_=src.rearrange("(p j) c -> p j c", j=PACK))
            return raw

        def load_pool_piece(name, pool, u, h):
            raw = alloc(f"{name}_raw{u}{h}", [P, 2, N], F32)
            rows = pool.rearrange("(p j) c -> p j c", j=PACK)
            nc.sync.dma_start(out=raw[:], in_=rows[:, 2 * u : 2 * u + 2, h * N : (h + 1) * N])
            return raw

        k_raw = {}
        v_raw = {}
        k_raw[0, 0] = load_pool_piece("k", kT, 0, 0)
        offsets = sb.tile([P, N // 16], U16, name="offsets")
        nc.sync.dma_start(offsets[:], offs)
        k_raw[0, 1] = load_pool_piece("k", kT, 0, 1)
        ts_pool = alloc("ts_pool", [P, T], F32)
        nc.sync.dma_start(out=ts_pool[0:32, :], in_=ts[0:32, :])
        rw_col = alloc("rw_col", [P, PACK], F32)
        nc.sync.dma_start(out=rw_col[:], in_=rw[0].rearrange("(s t) o -> s (t o)", t=PACK))
        for h in range(2):
            k_raw[1, h] = load_pool_piece("k", kT, 1, h)
        q_raw = load_rows("q_raw", qT[0])
        for h in range(2):
            v_raw[0, h] = load_pool_piece("v", vT, 0, h)
        dom_raw = load_rows("dom_raw", dom[0])
        for h in range(2):
            v_raw[1, h] = load_pool_piece("v", vT, 1, h)
        do_raw = load_rows("do_raw", doT[0])
        qm_raw = load_rows("qm_raw", qm[0])

        ident = alloc("ident", [P, P], F32)
        make_identity(nc, ident[:])
        nc.vector.memset(ts_pool[32:64, :], 0.0)
        nc.vector.memset(ts_pool[64:128, :], 0.0)
        warm = alloc("warm", [P, 2], F32)
        nc.vector.memset(warm[:, 0:1], 0.0)
        nc.scalar.activation(out=warm[:, 1:2], in_=warm[:, 0:1], func=ACT.Sigmoid)
        window = [alloc(f"window{w}", [P, T], F32) for w in range(4)]
        for w in range(4):
            nc.gpsimd.memset(window[w][:], 0.0)

        def operand(name, bf_tag="", codes_tag="", scales_tag=""):
            return (
                alloc(name + "_bf", [P, N * PACK], BF16, bf_tag),
                alloc(name + "_codes", [P, N], U32, codes_tag),
                alloc(name + "_scales", [P, N], U8, scales_tag),
            )

        def quantize(op, fmt, lo=0, hi=N):
            bf, codes, scales = op
            nc.vector.quantize_mx(out=codes[:, lo:hi].bitcast(fmt), scales=scales[:, lo:hi], in_=bf[:, lo * PACK : hi * PACK])

        def product(b, stat, stat_fmt, m, mov, mov_fmt):
            cols = slice(m * P, (m + 1) * P)
            nc.tensor.matmul_mx(
                out=bank[b][:],
                lhsT=stat[1][:, cols].bitcast(stat_fmt),
                lhsT_scale=stat[2][:, cols],
                rhs=mov[1][:].bitcast(mov_fmt),
                rhs_scale=mov[2][:],
                start=True,
                stop=True,
            )

        def scalar_move(dst, src):
            nc.scalar.activation(out=dst, in_=src, func=ACT.Copy)

        def gpsimd_cast(dst, src):
            nc.gpsimd.tensor_scalar(dst, src, 1.0, 0.0, ALU.mult, ALU.add)

        def cast_pairs(move, pairs, raw, h, lo=0, hi=N):
            dst = pairs[:, h * N + lo : h * N + hi].bitcast(BF16).rearrange("p (c e) -> p c e", e=2)
            move(dst, raw[:, :, lo:hi].rearrange("p e c -> p c e"))

        def gather(dst, pool):
            nc.vector.tensor_copy(dst, pool[:].indirect(offsets[:]))

        def weave(copy, word, op, listed, lo=0, hi=PACK):
            copy(
                op[0][:].bitcast(word).rearrange("p (t s u) -> p s t u", t=PACK, u=2)[:, :, lo:hi],
                listed[:].bitcast(word).rearrange("p (u s t) -> p s t u", u=2, t=PACK)[:, :, lo:hi],
            )

        def interleave(copy, bf, raw, lo, hi):
            dst = bf[:].rearrange("p (c i j) -> p c j i", i=PACK, j=PACK)
            src = raw[:].rearrange("p j (c i) -> p c j i", i=PACK)
            copy(dst[:, lo:hi], src[:, lo:hi])

        for t in range(PACK):
            nc.tensor.transpose(quarter(4, t), rw_col[:, t : t + 1].to_broadcast([P, P]), ident[:])
        ts_listed = alloc("ts_listed", [P, N], F32)
        gather(ts_listed[:], ts_pool)
        for t in range(PACK):
            nc.tensor.transpose(quarter(5, t), ts_listed[:, t:N:PACK], ident[:])

        k_pairs = [alloc(f"k_pairs{u}", [P, T], U32) for u in range(2)]
        k_listed = alloc("k_listed", [P, 2 * N], U32)
        k_op = operand("k")
        cast_pairs(scalar_move, k_pairs[0], k_raw[0, 0], 0)
        cast_pairs(scalar_move, k_pairs[0], k_raw[0, 1], 1)
        gather(k_listed[:, :N], k_pairs[0])
        cast_pairs(scalar_move, k_pairs[1], k_raw[1, 0], 0)
        cast_pairs(scalar_move, k_pairs[1], k_raw[1, 1], 1, 0, K_SPLIT)
        cast_pairs(nc.vector.tensor_copy, k_pairs[1], k_raw[1, 1], 1, K_SPLIT, N)
        gather(k_listed[:, N:], k_pairs[1])
        ts_col = alloc("ts_col", [P, PACK], F32)
        nc.scalar.copy(ts_col[:], bank[5][:, 0:N:P])
        for a in range(2):
            weave(nc.vector.tensor_copy, I32, k_op, k_listed, 2 * a, 2 * a + 2)
        for a in range(2):
            quantize(k_op, E4M3, a * HALF, (a + 1) * HALF)
        q_op = operand("q")
        q_dst = q_op[0][:].rearrange("p (t s j) -> p s j t", t=PACK, j=PACK)
        q_src = q_raw[:].rearrange("p j (s t) -> p s j t", t=PACK)
        nc.scalar.copy(q_dst[:, :Q_SPLIT], q_src[:, :Q_SPLIT])
        nc.vector.tensor_copy(q_dst[:, Q_SPLIT:], q_src[:, Q_SPLIT:])
        quantize(q_op, E4M3)

        prob_all = alloc("prob", [P, PACK * N], F32)
        pw32_all = alloc("pw32", [P, PACK * N], F32)
        prob = [prob_all[:, t * N : (t + 1) * N] for t in range(PACK)]
        pw32 = [pw32_all[:, t * N : (t + 1) * N] for t in range(PACK)]
        dom_op = operand("dom")
        dom_dst = dom_op[0][:].rearrange("p (c j) -> p c j", j=PACK)
        dom_src = dom_raw[:].rearrange("p j c -> p c j")
        for a in range(2):
            gpsimd_cast(dom_dst[:, a * HALF : (a + 1) * HALF], dom_src[:, a * HALF : (a + 1) * HALF])
        for t in range(PACK):
            product(t, k_op, E4M3, t, q_op, E4M3)
        for t in range(PACK):
            width = HALF if t == PACK - 1 else N
            for lo in range(0, N, width):
                cols = slice(lo, lo + width)
                nc.scalar.activation(out=prob[t][:, cols], in_=bank[t][:, cols], func=ACT.Sigmoid, scale=ts_col[:, t : t + 1])
                nc.vector.tensor_tensor(pw32[t][:, cols], prob[t][:, cols], bank[4][:, cols], ALU.mult)
        quantize(dom_op, E5M2)
        pw_op = operand("pw", scales_tag="dom_bf")
        for t in range(PACK):
            for j in range(PACK):
                nc.tensor.transpose(quarter(t, j), pw32[t][:, j * P : (j + 1) * P], ident[:])
            nc.scalar.copy(
                pw_op[0][:, t * N : (t + 1) * N].rearrange("s (p j) -> s p j", j=PACK),
                bank[t][:].rearrange("s (j p) -> s p j", j=PACK),
            )
            quantize(pw_op, E4M3, t * P, (t + 1) * P)

        stage = [alloc("stage0", [P, N], F32)]

        def to_list_order(m, b):
            nc.scalar.copy(stage[m][:].rearrange("e (p t) -> e p t", t=PACK), bank[b][:].rearrange("e (t p) -> e p t", t=PACK))

        def scatter(i, out, m):
            nc.vector.tensor_copy(window[m][:].indirect(offsets[:]), stage[i][:])
            nc.sync.dma_start(out=out[m * P : (m + 1) * P, :], in_=window[m][:])

        for m, b in enumerate((5, 6, 4)):
            product(b, dom_op, E5M2, m, pw_op, E4M3)
        to_list_order(0, 5)

        v_pairs = [alloc("v_pairs0", [P, T], U32), alloc("v_pairs1", [P, T], U32, "pw_bf")]
        v_listed = alloc("v_listed", [P, 2 * N], U32)
        v_op = operand("v")
        for h in range(2):
            cast_pairs(scalar_move, v_pairs[0], v_raw[0, h], h)
        gather(v_listed[:, :N], v_pairs[0])
        cast_pairs(scalar_move, v_pairs[1], v_raw[1, 0], 0, 0, V_SPLIT)
        cast_pairs(nc.vector.tensor_copy, v_pairs[1], v_raw[1, 0], 0, V_SPLIT, N)
        cast_pairs(nc.vector.tensor_copy, v_pairs[1], v_raw[1, 1], 1)
        gather(v_listed[:, N:], v_pairs[1])
        scatter(0, out_2, 0)
        rest = alloc("rest", [P, PACK * N], F32, "v_raw11")
        nc.gpsimd.tensor_scalar(rest[:], prob_all[:], -1.0, 1.0, ALU.mult, ALU.add)

        def slopes(both, first):
            cols = slice(first * N, (first + 2) * N)
            nc.gpsimd.tensor_tensor(both[:], rest[:, cols], pw32_all[:, cols], ALU.mult)
            return [both[:, :N], both[:, N:]]

        slope = slopes(alloc("slope01", [P, 2 * N], F32), 0)
        do_op = operand("do")
        do_dst = do_op[0][:].rearrange("p (u s e j) -> p s j u e", u=2, e=2, j=PACK)
        do_src = do_raw[:].rearrange("p j (s u e) -> p s j u e", u=2, e=2)
        qm_bf = alloc("qm_bf", [P, N * PACK], BF16)
        weave(nc.scalar.copy, U32, v_op, v_listed)
        quantize(v_op, E4M3)
        for a in range(2):
            nc.scalar.copy(do_dst[:, a * 64 : (a + 1) * 64], do_src[:, a * 64 : (a + 1) * 64])
        quantize(do_op, E5M2)
        slope.extend(slopes(alloc("slope23", [P, 2 * N], F32, "do_bf"), 2))
        stage.append(alloc("stage1", [P, N], F32, "do_raw"))
        to_list_order(1, 6)
        scatter(1, out_2, 1)
        for a in range(2):
            interleave(nc.scalar.copy, qm_bf, qm_raw, a * 64, (a + 1) * 64)

        ds_flat = alloc("ds", [P, PACK * N], BF16)
        ds = ds_flat[:].rearrange("p (t c) -> p t c", t=PACK)
        for t in range(PACK):
            product(t, v_op, E4M3, t, do_op, E5M2)
        for t in range(GPSIMD_TILES):
            scaled = alloc(f"scaled{t}", [P, N], F32)
            nc.scalar.activation(out=scaled[:], in_=bank[t][:], func=ACT.Copy, scale=ts_col[:, t : t + 1])
            nc.gpsimd.tensor_tensor(
                ds[:, t, :].rearrange("p (u s e) -> p u s e", u=2, e=2),
                scaled[:].rearrange("p (u s e) -> p u s e", u=2, e=2),
                slope[t].rearrange("p (u e s) -> p u s e", u=2, e=2),
                ALU.mult,
            )
        for t in range(GPSIMD_TILES, PACK):
            for u in range(2):
                half = slice(u * HALF, (u + 1) * HALF)
                nc.vector.scalar_tensor_tensor(
                    ds[:, t, half].rearrange("p (s e) -> p s e", e=2),
                    bank[t][:, half].rearrange("p (s e) -> p s e", e=2),
                    ts_col[:, t : t + 1],
                    slope[t][:, half].rearrange("p (e s) -> p s e", e=2),
                    ALU.mult,
                    ALU.mult,
                )
        stage.append(alloc("stage2", [P, N], F32, "v_raw11"))
        stage.append(alloc("stage3", [P, N], F32))
        to_list_order(2, 4)
        scatter(2, out_2, 2)
        qm_op = (qm_bf, alloc("qm_codes", [P, N], U32, "v_raw11"), alloc("qm_scales", [P, N], U8))
        quantize(qm_op, E4M3)

        kt_op = operand("kt", codes_tag="qm_bf")
        k_words = k_op[0][:].bitcast(F32).rearrange("p (t s u) -> p t u s", t=PACK, u=2)
        for u in range(2):
            for t in range(PACK):
                nc.tensor.transpose(quarter(5 + u, t), k_words[:, t, u, :], ident[:])
            nc.scalar.copy(
                kt_op[0][:].rearrange("s (p u e t) -> s u p e t", u=2, e=2, t=PACK)[:, u],
                bank[5 + u][:].bitcast(BF16).rearrange("s (t p e) -> s p e t", t=PACK, e=2),
            )
        quantize(kt_op, E4M3)

        dsr_op = operand("dsr")
        for h, b in ((0, 7), (1, 4)):
            for t2 in range(2):
                words = ds_flat[:, (2 * h + t2) * N : (2 * h + t2 + 1) * N].bitcast(F32)
                for u in range(2):
                    nc.tensor.transpose(quarter(b, 2 * t2 + u), words[:, u * P : (u + 1) * P], ident[:])
            nc.scalar.copy(
                dsr_op[0][:, h * 1024 : (h + 1) * 1024].bitcast(F32).rearrange("s (t p u) -> s t p u", t=2, u=2),
                bank[b][:].rearrange("s (t u p) -> s t p u", t=2, u=2),
            )
        quantize(dsr_op, E5M2)
        product(7, dom_op, E5M2, 3, pw_op, E4M3)
        to_list_order(3, 7)
        scatter(3, out_2, 3)

        dss_op = operand("dss", bf_tag="dsr_bf")
        dss_dst = dss_op[0][:].rearrange("p (u e s t) -> p u s t e", u=2, e=2, t=PACK)
        dss_src = ds_flat[:].rearrange("p (t u s e) -> p u s t e", t=PACK, u=2, e=2)
        for u in range(2):
            for a in range(2):
                nc.scalar.copy(dss_dst[:, u, a * 64 : (a + 1) * 64], dss_src[:, u, a * 64 : (a + 1) * 64])
        quantize(dss_op, E5M2)

        for m in range(PACK):
            product(1 + m, qm_op, E4M3, m, dsr_op, E5M2)
            stage.append(alloc(f"stage{PACK + m}", [P, N], F32))
            to_list_order(PACK + m, 1 + m)
            scatter(PACK + m, out_1, m)

        gq = alloc("gq", [P, PACK, N], F32)
        gq_bank = (5, 6, 7, 0)
        rows = out_0[0].rearrange("(s m) d -> s m d", m=PACK)
        for m in range(PACK):
            product(gq_bank[m], dss_op, E5M2, m, kt_op, E4M3)
            nc.scalar.copy(gq[:, m, :], bank[gq_bank[m]][:])
            if m % 2 == 1:
                nc.scalar.dma_start(out=rows[:, m - 1 : m + 1, :], in_=gq[:, m - 1 : m + 1, :])
